import numpy as np
import ml_dtypes


def mxq(x, axis, fmt="e4m3"):
    dtype, down = {"e4m3": (ml_dtypes.float8_e4m3fn, 7), "e5m2": (ml_dtypes.float8_e5m2, 14)}[fmt]
    v = np.moveaxis(np.asarray(x, np.float32).astype(ml_dtypes.bfloat16).astype(np.float64), axis, -1)
    blocks = v.reshape(v.shape[:-1] + (-1, 32))
    amax = np.abs(blocks).max(-1, keepdims=True)
    byte = np.maximum(np.where(amax > 0, np.frexp(amax)[1] - 1 + 127, 0) - down, 1)
    scale = np.exp2(byte - 127.0)
    codes = (blocks / scale).astype(np.float32).astype(dtype).astype(np.float64)
    return np.moveaxis((codes * scale).reshape(v.shape), -1, axis)


WIDE = False


def mx_kscale(k):
    if not WIDE:
        return np.ones(k)
    levels = np.array([10, -10, 5, -5, 0])
    if k % 512:
        return np.exp2(np.random.permutation(np.resize(levels, k // 32))).repeat(32)
    a = np.empty((k // 512, 16))
    for p in range(k // 512):
        a[p, :8] = np.random.permutation(np.resize(levels, 8))
        for g in range(8):
            far = levels[np.abs(levels - a[p, g]) >= 10]
            a[p, g + 8] = far[np.random.randint(len(far))]
    return np.exp2(a.ravel()).repeat(32)


def f64(x):
    return np.asarray(x).astype(np.float64)


def striped(idx):
    return np.tile(idx.reshape(-1, 16).T, (8, 1)).astype(np.uint16)


def unstriped(offs):
    return offs[:16].T.reshape(-1).astype(np.int64)


K, T, E, C, N = 1536, 1024, 8, 256, 128


def by_expert(wq, xq):
    return np.concatenate([wq[e].T @ xq[:, e * C:(e + 1) * C] for e in range(E)], axis=1)


def setup_inputs():
    n = np.random.standard_normal
    s = mx_kscale(K)[:, None]
    first = np.random.permutation(np.repeat(np.arange(E), T // E))
    second = (first + 1 + np.random.permutation(np.repeat(np.arange(E - 1), -(-T // (E - 1)))[:T])) % E
    while np.bincount(second, minlength=E).max() != T // E:
        load = np.bincount(second, minlength=E); hi, lo = int(load.argmax()), int(load.argmin())
        t = np.flatnonzero((second == hi) & (first != lo))[0]; second[t] = lo
    slot_token = np.empty(E * C, np.int64); pos = np.empty((2, T), np.int64); fill = np.zeros(E, np.int64)
    place = np.stack([np.random.permutation(C) for _ in range(E)])
    for r, deal in enumerate((first, second)):
        for t in np.random.permutation(T):
            e = deal[t]; j = e * C + place[e, fill[e]]; fill[e] += 1; slot_token[j] = t; pos[r, t] = j
    g = np.random.uniform(0.2, 0.8, T)
    return {
        "xT": (n((K, T)) * s).astype(np.float32),
        "w": (n((E, K, N)) / np.sqrt(K) / s[None]).astype(np.float32),
        "gate": np.stack([np.tile(g, (N, 1)), np.tile(1.0 - g, (N, 1))]).astype(np.float32),
        "offs": striped(slot_token),
        "pos1": striped(pos[0]),
        "pos2": striped(pos[1]),
    }


def reference(xT, w, gate, offs, pos1, pos2):
    idx = unstriped(offs)
    xq = mxq(f64(xT)[:, idx], 0, "e4m3")
    y = by_expert(mxq(f64(w), 1, "e4m3"), xq)
    return f64(gate[0]) * y[:, unstriped(pos1)] + f64(gate[1]) * y[:, unstriped(pos2)]

@@ -1,0 +1,159 @@
+from contextlib import ExitStack
+
+import concourse.mybir as mybir
+
+K, T, E, C, N = 1536, 1024, 8, 256, 128
+FLOPS = 2 * K * N * E * C
+
+F32 = mybir.dt.float32
+BF16 = mybir.dt.bfloat16
+U32 = mybir.dt.uint32
+U16 = mybir.dt.uint16
+U8 = mybir.dt.uint8
+FP8X4 = mybir.dt.float8_e4m3fn_x4
+MULT = mybir.AluOpType.mult
+ADD = mybir.AluOpType.add
+
+P = 128
+PASSES = K // 512
+UNITS = E * PASSES
+
+
+def tile_routed_moe_kernel(tc, xT, w, gate, offs, pos1, pos2, out):
+    nc = tc.nc
+    with ExitStack() as ctx:
+        keep = ctx.enter_context(tc.tile_pool(name="keep", bufs=1))
+        psum = ctx.enter_context(tc.psum_pool(name="psum", bufs=1))
+
+        offs_sb = keep.tile([P, E * C // 16], U16, name="offs_sb")
+        pos1_sb = keep.tile([P, T // 16], U16, name="pos1_sb")
+        pos2_sb = keep.tile([P, T // 16], U16, name="pos2_sb")
+
+        x_view = xT.rearrange("(a p j) n -> a p j n", p=P, j=4)
+        w_view = w.rearrange("e (a p j) n -> p (e a) j n", p=P, j=4)
+
+        chunks = [(0, 0, 256, "s"), (0, 256, 256, "s"), (0, 512, 256, "v"), (0, 768, 256, "v")]
+        for a in (1, 2):
+            chunks += [(a, 0, 512, "s"), (a, 512, 512, "s")]
+        w_chunks = [(0, 4), (4, 4), (8, 4), (12, 4), (16, 4), (20, 2), (22, 2)]
+
+        x_raw = []
+        for i, (a, t0, n, eng) in enumerate(chunks):
+            raw = keep.tile([P, 4, n], F32, name=f"x_raw{i}")
+            nc.sync.dma_start(out=raw[:], in_=x_view[a, :, :, t0 : t0 + n])
+            x_raw.append(raw)
+            if i == 1:
+                nc.sync.dma_start(offs_sb[:], offs)
+        w_raw = []
+        for i, (u0, n) in enumerate(w_chunks):
+            raw = keep.tile([P, n, 4, N], F32, name=f"w_raw{i}")
+            nc.sync.dma_start(out=raw[:], in_=w_view[:, u0 : u0 + n, :, :])
+            w_raw.append(raw)
+        nc.sync.dma_start(pos1_sb[:], pos1)
+        nc.sync.dma_start(pos2_sb[:], pos2)
+        gates = []
+        for r in range(2):
+            g = keep.tile([P, T], F32, name=f"gate{r}")
+            nc.sync.dma_start(out=g[:], in_=gate[r, :, :])
+            gates.append(g)
+
+        words = [keep.tile([P, T], U32, align_bytes=64, name=f"words{a}") for a in range(PASSES)]
+        planes = keep.tile([P, T], U8, align_bytes=64, name="planes")
+        nc.gpsimd.memset(planes[:], 0)
+
+        slot_words = keep.tile([P, PASSES, E * C], U32, align_bytes=64, name="slot_words")
+        slot_planes = keep.tile([P, E * C], U8, align_bytes=64, name="slot_planes")
+        w_codes = keep.tile([P, UNITS, N], U32, align_bytes=64, name="w_codes")
+        w_scales = keep.tile([P, UNITS, N], U8, align_bytes=64, name="w_scales")
+
+        def copy(eng, dst, src):
+            if eng == "v":
+                nc.vector.tensor_copy(out=dst, in_=src)
+            elif eng == "g":
+                nc.gpsimd.tensor_copy(out=dst, in_=src)
+            else:
+                nc.scalar.copy(out=dst, in_=src)
+
+        def tokens(i):
+            a, t0, n, eng = chunks[i]
+            grouped = keep.tile([P, n * 4], BF16, align_bytes=64, name=f"x_grouped{i}")
+            copy(
+                eng,
+                grouped[:].rearrange("p (c i j) -> p c j i", i=4, j=4),
+                x_raw[i][:].rearrange("p j (c i) -> p c j i", i=4),
+            )
+            nc.vector.quantize_mx(
+                out=words[a][:, t0 : t0 + n].bitcast(FP8X4),
+                scales=planes[4 * a : P, t0 : t0 + n],
+                in_=grouped[:],
+            )
+
+        def gather_words(a, cuts):
+            for s, n in cuts:
+                nc.vector.tensor_copy(
+                    out=slot_words[:, a, s : s + n],
+                    in_=words[a][:].indirect(offs_sb[:, s // 16 : (s + n) // 16]),
+                )
+
+        def weights(i):
+            u0, n = w_chunks[i]
+            grouped = keep.tile([P, n * N * 4], BF16, align_bytes=64, name=f"w_grouped{i}")
+            copy(
+                "s",
+                grouped[:].rearrange("p (u c i j) -> p u c j i", u=n, i=4, j=4),
+                w_raw[i][:].rearrange("p u j (c i) -> p u c j i", i=4),
+            )
+            nc.vector.quantize_mx(
+                out=w_codes[:, u0 : u0 + n, :].rearrange("p u n -> p (u n)").bitcast(FP8X4),
+                scales=w_scales[:, u0 : u0 + n, :].rearrange("p u n -> p (u n)"),
+                in_=grouped[:],
+            )
+
+        THREE = [(0, 768), (768, 768), (1536, 512)]
+        FOUR = [(0, 768), (768, 768), (1536, 256), (1792, 256)]
+        for i in range(4):
+            tokens(i)
+        gather_words(0, THREE)
+        tokens(4)
+        tokens(5)
+        gather_words(1, THREE)
+        tokens(6)
+        tokens(7)
+        for s, n in THREE:
+            nc.vector.tensor_copy(
+                out=slot_planes[:, s : s + n],
+                in_=planes[:].indirect(offs_sb[:, s // 16 : (s + n) // 16]),
+            )
+        for i in range(len(w_chunks)):
+            weights(i)
+        gather_words(2, FOUR)
+
+        y = keep.tile([P, E * C], F32, name="y")
+        accs = [psum.tile([P, C], F32, name=f"acc{e}") for e in range(E)]
+        for a in range(PASSES):
+            for e in range(E):
+                acc = accs[e]
+                cols = slice(e * C, (e + 1) * C)
+                u = e * PASSES + a
+                nc.tensor.matmul_mx(
+                    out=acc[:],
+                    lhsT=w_codes[:, u, :].bitcast(FP8X4),
+                    lhsT_scale=w_scales[:, u, :],
+                    rhs=slot_words[:, a, cols].bitcast(FP8X4),
+                    rhs_scale=slot_planes[4 * a : P, cols],
+                    start=(a == 0),
+                    stop=(a == PASSES - 1),
+                )
+                if a == PASSES - 1:
+                    nc.scalar.copy(out=y[:, cols], in_=acc[:])
+
+        for i, t0 in enumerate(range(0, T, 512)):
+            first = keep.tile([P, 512], F32, name=f"first{i}")
+            second = keep.tile([P, 512], F32, name=f"second{i}")
+            total = keep.tile([P, 512], F32, name=f"total{i}")
+            for dst, pos_sb, g in ((first, pos1_sb, gates[0]), (second, pos2_sb, gates[1])):
+                nc.vector.tensor_tensor(
+                    dst[:], y[:].indirect(pos_sb[:, t0 // 16 : (t0 + 512) // 16]), g[:, t0 : t0 + 512], MULT
+                )
+            nc.vector.tensor_tensor(total[:], first[:], second[:], ADD)
+            nc.sync.dma_start(out=out[:, t0 : t0 + 512], in_=total[:])

@@ -46,7 +46,7 @@ def tile_routed_moe_kernel(tc, xT, w, gate, offs, pos1, pos2, out):
                 nc.sync.dma_start(offs_sb[:], offs)
         w_raw = []
         for i, (u0, n) in enumerate(w_chunks):
-            raw = keep.tile([P, n, 4, N], F32, name=f"w_raw{i}")
+            raw = keep.tile([P, n, 4, N], F32, name=f"w_raw{i}", tag="late" if i == len(w_chunks) - 1 else f"w_raw{i}")
             nc.sync.dma_start(out=raw[:], in_=w_view[:, u0 : u0 + n, :, :])
             w_raw.append(raw)
         nc.sync.dma_start(pos1_sb[:], pos1)
@@ -74,18 +74,31 @@ def tile_routed_moe_kernel(tc, xT, w, gate, offs, pos1, pos2, out):
             else:
                 nc.scalar.copy(out=dst, in_=src)
 
-        def tokens(i):
-            a, t0, n, eng = chunks[i]
+        x_grouped = []
+        for i, (a, t0, n, eng) in enumerate(chunks):
             grouped = keep.tile([P, n * 4], BF16, align_bytes=64, name=f"x_grouped{i}")
             copy(
                 eng,
                 grouped[:].rearrange("p (c i j) -> p c j i", i=4, j=4),
                 x_raw[i][:].rearrange("p j (c i) -> p c j i", i=4),
             )
+            x_grouped.append(grouped)
+        w_grouped = []
+        for i, (u0, n) in enumerate(w_chunks):
+            grouped = keep.tile([P, n * N * 4], BF16, align_bytes=64, name=f"w_grouped{i}")
+            copy(
+                "s",
+                grouped[:].rearrange("p (u c i j) -> p u c j i", u=n, i=4, j=4),
+                w_raw[i][:].rearrange("p u j (c i) -> p u c j i", i=4),
+            )
+            w_grouped.append(grouped)
+
+        def tokens(i):
+            a, t0, n, eng = chunks[i]
             nc.vector.quantize_mx(
                 out=words[a][:, t0 : t0 + n].bitcast(FP8X4),
                 scales=planes[4 * a : P, t0 : t0 + n],
-                in_=grouped[:],
+                in_=x_grouped[i][:],
             )
 
         def gather_words(a, cuts):
@@ -97,16 +110,10 @@ def tile_routed_moe_kernel(tc, xT, w, gate, offs, pos1, pos2, out):
 
         def weights(i):
             u0, n = w_chunks[i]
-            grouped = keep.tile([P, n * N * 4], BF16, align_bytes=64, name=f"w_grouped{i}")
-            copy(
-                "s",
-                grouped[:].rearrange("p (u c i j) -> p u c j i", u=n, i=4, j=4),
-                w_raw[i][:].rearrange("p u j (c i) -> p u c j i", i=4),
-            )
             nc.vector.quantize_mx(
                 out=w_codes[:, u0 : u0 + n, :].rearrange("p u n -> p (u n)").bitcast(FP8X4),
                 scales=w_scales[:, u0 : u0 + n, :].rearrange("p u n -> p (u n)"),
-                in_=grouped[:],
+                in_=w_grouped[i][:],
             )
 
         THREE = [(0, 768), (768, 768), (1536, 512)]
@@ -128,7 +135,7 @@ def tile_routed_moe_kernel(tc, xT, w, gate, offs, pos1, pos2, out):
             weights(i)
         gather_words(2, FOUR)
 
-        y = keep.tile([P, E * C], F32, name="y")
+        y = keep.tile([P, E * C], F32, name="y", tag="late")
         accs = [psum.tile([P, C], F32, name=f"acc{e}") for e in range(E)]
         for a in range(PASSES):
             for e in range(E):

@@ -33,6 +33,7 @@ def tile_routed_moe_kernel(tc, xT, w, gate, offs, pos1, pos2, out):
         w_view = w.rearrange("e (a p j) n -> p (e a) j n", p=P, j=4)
 
         chunks = [(0, 0, 256, "s"), (0, 256, 256, "s"), (0, 512, 256, "v"), (0, 768, 256, "v")]
+        gpsimd_chunks = (0, 2)
         for a in (1, 2):
             chunks += [(a, 0, 512, "s"), (a, 512, 512, "s")]
         w_chunks = [(0, 4), (4, 4), (8, 4), (12, 4), (16, 4), (20, 2), (22, 2)]
@@ -86,11 +87,21 @@ def tile_routed_moe_kernel(tc, xT, w, gate, offs, pos1, pos2, out):
         w_grouped = []
         for i, (u0, n) in enumerate(w_chunks):
             grouped = keep.tile([P, n * N * 4], BF16, align_bytes=64, name=f"w_grouped{i}")
-            copy(
-                "s",
-                grouped[:].rearrange("p (u c i j) -> p u c j i", u=n, i=4, j=4),
-                w_raw[i][:].rearrange("p u j (c i) -> p u c j i", i=4),
-            )
+            if i in gpsimd_chunks:
+                for u in range(n):
+                    nc.gpsimd.tensor_scalar(
+                        out=grouped[:, u * 4 * N : (u + 1) * 4 * N].rearrange("p (c i j) -> p c j i", i=4, j=4),
+                        in0=w_raw[i][:, u, :, :].rearrange("p j (c i) -> p c j i", i=4),
+                        scalar1=1.0,
+                        scalar2=0.0,
+                        op0=MULT,
+                        op1=ADD,
+                    )
+            else:
+                nc.scalar.copy(
+                    out=grouped[:].rearrange("p (u c i j) -> p u c j i", u=n, i=4, j=4),
+                    in_=w_raw[i][:].rearrange("p u j (c i) -> p u c j i", i=4),
+                )
             w_grouped.append(grouped)
 
         def tokens(i):
@@ -154,13 +165,13 @@ def tile_routed_moe_kernel(tc, xT, w, gate, offs, pos1, pos2, out):
                 if a == PASSES - 1:
                     nc.scalar.copy(out=y[:, cols], in_=acc[:])
 
-        for i, t0 in enumerate(range(0, T, 512)):
-            first = keep.tile([P, 512], F32, name=f"first{i}")
-            second = keep.tile([P, 512], F32, name=f"second{i}")
-            total = keep.tile([P, 512], F32, name=f"total{i}")
+        for i, (t0, n) in enumerate([(0, 768), (768, 256)]):
+            first = keep.tile([P, n], F32, name=f"first{i}")
+            second = keep.tile([P, n], F32, name=f"second{i}")
+            total = keep.tile([P, n], F32, name=f"total{i}")
             for dst, pos_sb, g in ((first, pos1_sb, gates[0]), (second, pos2_sb, gates[1])):
                 nc.vector.tensor_tensor(
-                    dst[:], y[:].indirect(pos_sb[:, t0 // 16 : (t0 + 512) // 16]), g[:, t0 : t0 + 512], MULT
+                    dst[:], y[:].indirect(pos_sb[:, t0 // 16 : (t0 + n) // 16]), g[:, t0 : t0 + n], MULT
                 )
             nc.vector.tensor_tensor(total[:], first[:], second[:], ADD)
-            nc.sync.dma_start(out=out[:, t0 : t0 + 512], in_=total[:])
+            nc.sync.dma_start(out=out[:, t0 : t0 + n], in_=total[:])

from contextlib import ExitStack

import concourse.mybir as mybir

K, T, E, C, N = 1536, 1024, 8, 256, 128
FLOPS = 2 * K * N * E * C

F32 = mybir.dt.float32
BF16 = mybir.dt.bfloat16
U32 = mybir.dt.uint32
U16 = mybir.dt.uint16
U8 = mybir.dt.uint8
FP8X4 = mybir.dt.float8_e4m3fn_x4
MULT = mybir.AluOpType.mult
ADD = mybir.AluOpType.add

P = 128
PASSES = K // 512
UNITS = E * PASSES


def tile_routed_moe_kernel(tc, xT, w, gate, offs, pos1, pos2, out):
    nc = tc.nc
    with ExitStack() as ctx:
        keep = ctx.enter_context(tc.tile_pool(name="keep", bufs=1))
        psum = ctx.enter_context(tc.psum_pool(name="psum", bufs=1))

        offs_sb = keep.tile([P, E * C // 16], U16, name="offs_sb")
        pos1_sb = keep.tile([P, T // 16], U16, name="pos1_sb")
        pos2_sb = keep.tile([P, T // 16], U16, name="pos2_sb")

        x_view = xT.rearrange("(a p j) n -> a p j n", p=P, j=4)
        w_view = w.rearrange("e (a p j) n -> p (e a) j n", p=P, j=4)

        chunks = [(0, 0, 256, "s"), (0, 256, 256, "s"), (0, 512, 256, "v"), (0, 768, 256, "v")]
        gpsimd_chunks = (0, 2)
        for a in (1, 2):
            chunks += [(a, 0, 512, "s"), (a, 512, 512, "s")]
        w_chunks = [(0, 4), (4, 4), (8, 4), (12, 4), (16, 4), (20, 2), (22, 2)]

        x_raw = []
        for i, (a, t0, n, eng) in enumerate(chunks):
            raw = keep.tile([P, 4, n], F32, name=f"x_raw{i}")
            nc.sync.dma_start(out=raw[:], in_=x_view[a, :, :, t0 : t0 + n])
            x_raw.append(raw)
            if i == 1:
                nc.sync.dma_start(offs_sb[:], offs)
        w_raw = []
        for i, (u0, n) in enumerate(w_chunks):
            raw = keep.tile([P, n, 4, N], F32, name=f"w_raw{i}", tag="late" if i == len(w_chunks) - 1 else f"w_raw{i}")
            nc.sync.dma_start(out=raw[:], in_=w_view[:, u0 : u0 + n, :, :])
            w_raw.append(raw)
        nc.sync.dma_start(pos1_sb[:], pos1)
        nc.sync.dma_start(pos2_sb[:], pos2)
        gates = []
        for r in range(2):
            g = keep.tile([P, T], F32, name=f"gate{r}")
            nc.sync.dma_start(out=g[:], in_=gate[r, :, :])
            gates.append(g)

        words = [keep.tile([P, T], U32, align_bytes=64, name=f"words{a}") for a in range(PASSES)]
        planes = keep.tile([P, T], U8, align_bytes=64, name="planes")
        nc.gpsimd.memset(planes[:], 0)

        slot_words = keep.tile([P, PASSES, E * C], U32, align_bytes=64, name="slot_words")
        slot_planes = keep.tile([P, E * C], U8, align_bytes=64, name="slot_planes")
        w_codes = keep.tile([P, UNITS, N], U32, align_bytes=64, name="w_codes")
        w_scales = keep.tile([P, UNITS, N], U8, align_bytes=64, name="w_scales")

        def copy(eng, dst, src):
            if eng == "v":
                nc.vector.tensor_copy(out=dst, in_=src)
            elif eng == "g":
                nc.gpsimd.tensor_copy(out=dst, in_=src)
            else:
                nc.scalar.copy(out=dst, in_=src)

        x_grouped = []
        for i, (a, t0, n, eng) in enumerate(chunks):
            grouped = keep.tile([P, n * 4], BF16, align_bytes=64, name=f"x_grouped{i}")
            copy(
                eng,
                grouped[:].rearrange("p (c i j) -> p c j i", i=4, j=4),
                x_raw[i][:].rearrange("p j (c i) -> p c j i", i=4),
            )
            x_grouped.append(grouped)
        w_grouped = []
        for i, (u0, n) in enumerate(w_chunks):
            grouped = keep.tile([P, n * N * 4], BF16, align_bytes=64, name=f"w_grouped{i}")
            if i in gpsimd_chunks:
                for u in range(n):
                    nc.gpsimd.tensor_scalar(
                        out=grouped[:, u * 4 * N : (u + 1) * 4 * N].rearrange("p (c i j) -> p c j i", i=4, j=4),
                        in0=w_raw[i][:, u, :, :].rearrange("p j (c i) -> p c j i", i=4),
                        scalar1=1.0,
                        scalar2=0.0,
                        op0=MULT,
                        op1=ADD,
                    )
            else:
                nc.scalar.copy(
                    out=grouped[:].rearrange("p (u c i j) -> p u c j i", u=n, i=4, j=4),
                    in_=w_raw[i][:].rearrange("p u j (c i) -> p u c j i", i=4),
                )
            w_grouped.append(grouped)

        def tokens(i):
            a, t0, n, eng = chunks[i]
            nc.vector.quantize_mx(
                out=words[a][:, t0 : t0 + n].bitcast(FP8X4),
                scales=planes[4 * a : P, t0 : t0 + n],
                in_=x_grouped[i][:],
            )

        def gather_words(a, cuts):
            for s, n in cuts:
                nc.vector.tensor_copy(
                    out=slot_words[:, a, s : s + n],
                    in_=words[a][:].indirect(offs_sb[:, s // 16 : (s + n) // 16]),
                )

        def weights(i):
            u0, n = w_chunks[i]
            nc.vector.quantize_mx(
                out=w_codes[:, u0 : u0 + n, :].rearrange("p u n -> p (u n)").bitcast(FP8X4),
                scales=w_scales[:, u0 : u0 + n, :].rearrange("p u n -> p (u n)"),
                in_=w_grouped[i][:],
            )

        THREE = [(0, 768), (768, 768), (1536, 512)]
        FOUR = [(0, 768), (768, 768), (1536, 256), (1792, 256)]
        for i in range(4):
            tokens(i)
        gather_words(0, THREE)
        tokens(4)
        tokens(5)
        gather_words(1, THREE)
        tokens(6)
        tokens(7)
        for s, n in THREE:
            nc.vector.tensor_copy(
                out=slot_planes[:, s : s + n],
                in_=planes[:].indirect(offs_sb[:, s // 16 : (s + n) // 16]),
            )
        for i in range(len(w_chunks)):
            weights(i)
        gather_words(2, FOUR)

        y = keep.tile([P, E * C], F32, name="y", tag="late")
        accs = [psum.tile([P, C], F32, name=f"acc{e}") for e in range(E)]
        for a in range(PASSES):
            for e in range(E):
                acc = accs[e]
                cols = slice(e * C, (e + 1) * C)
                u = e * PASSES + a
                nc.tensor.matmul_mx(
                    out=acc[:],
                    lhsT=w_codes[:, u, :].bitcast(FP8X4),
                    lhsT_scale=w_scales[:, u, :],
                    rhs=slot_words[:, a, cols].bitcast(FP8X4),
                    rhs_scale=slot_planes[4 * a : P, cols],
                    start=(a == 0),
                    stop=(a == PASSES - 1),
                )
                if a == PASSES - 1:
                    nc.scalar.copy(out=y[:, cols], in_=acc[:])

        for i, (t0, n) in enumerate([(0, 768), (768, 256)]):
            first = keep.tile([P, n], F32, name=f"first{i}")
            second = keep.tile([P, n], F32, name=f"second{i}")
            total = keep.tile([P, n], F32, name=f"total{i}")
            for dst, pos_sb, g in ((first, pos1_sb, gates[0]), (second, pos2_sb, gates[1])):
                nc.vector.tensor_tensor(
                    dst[:], y[:].indirect(pos_sb[:, t0 // 16 : (t0 + n) // 16]), g[:, t0 : t0 + n], MULT
                )
            nc.vector.tensor_tensor(total[:], first[:], second[:], ADD)
            nc.sync.dma_start(out=out[:, t0 : t0 + n], in_=total[:])
